import numpy as np
import ml_dtypes


def mxq(x, axis, fmt="e4m3"):
    dtype, down = {"e4m3": (ml_dtypes.float8_e4m3fn, 7), "e5m2": (ml_dtypes.float8_e5m2, 14)}[fmt]
    v = np.moveaxis(np.asarray(x, np.float32).astype(ml_dtypes.bfloat16).astype(np.float64), axis, -1)
    blocks = v.reshape(v.shape[:-1] + (-1, 32))
    amax = np.abs(blocks).max(-1, keepdims=True)
    byte = np.maximum(np.where(amax > 0, np.frexp(amax)[1] - 1 + 127, 0) - down, 1)
    scale = np.exp2(byte - 127.0)
    codes = (blocks / scale).astype(np.float32).astype(dtype).astype(np.float64)
    return np.moveaxis((codes * scale).reshape(v.shape), -1, axis)


WIDE = False


def mx_kscale(k):
    if not WIDE:
        return np.ones(k)
    levels = np.array([30, -30])
    if k % 512:
        return np.exp2(np.random.permutation(np.resize(levels, k // 32))).repeat(32)
    a = np.empty((k // 512, 16))
    for p in range(k // 512):
        a[p, :8] = np.random.permutation(np.resize(levels, 8))
        for g in range(8):
            far = levels[np.abs(levels - a[p, g]) >= 10]
            a[p, g + 8] = far[np.random.randint(len(far))]
    return np.exp2(a.ravel()).repeat(32)


def f64(x):
    return np.asarray(x).astype(np.float64)


def striped(idx):
    return np.tile(np.asarray(idx).reshape(-1, 16).T, (8, 1)).astype(np.uint16)


def unstriped(offs):
    return offs[:16].T.reshape(-1).astype(np.int64)


E2M1 = np.array([0.0, 0.5, 1.0, 1.5, 2.0, 3.0, 4.0, 6.0, -0.0, -0.5, -1.0, -1.5, -2.0, -3.0, -4.0, -6.0])


def pack_weight(w, fmt):
    k, n = w.shape
    w = f64(np.asarray(w, np.float32).astype(ml_dtypes.bfloat16)).reshape(k // 32, 32, n)
    amax = np.abs(w).max(1)
    if fmt in ("e4m3", "e5m2"):
        byte = np.frexp(amax)[1] - 1 + 127 - (7 if fmt == "e4m3" else 14)
    else:
        mant, ex = np.frexp(amax / 6.0)
        byte = np.where(mant > 0.5, ex, ex - 1) + 127
    byte = np.clip(np.where(amax > 0, byte, 1), 1, 254)
    scaled = (w * np.exp2(127.0 - byte)[:, None, :]).reshape(k, n).astype(np.float32)
    by_word = np.ascontiguousarray(scaled.reshape(k // 512, 128, 4, n).transpose(0, 1, 3, 2))
    if fmt in ("e4m3", "e5m2"):
        words = by_word.astype(ml_dtypes.float8_e4m3fn if fmt == "e4m3" else ml_dtypes.float8_e5m2).view(np.uint8)
    else:
        c = by_word.astype(ml_dtypes.float4_e2m1fn).view(np.uint8) & 0xF
        words = (c[..., 0::2] | (c[..., 1::2] << 4)).reshape(k // 512, 128, 2 * n)
    return np.ascontiguousarray(words), np.ascontiguousarray(byte.astype(np.uint8).reshape(k // 512, 16, n))


def unpack_weight(words, scales, fmt):
    g, _, n = scales.shape
    words = np.ascontiguousarray(words).reshape(g, 128, n, -1)
    if fmt in ("e4m3", "e5m2"):
        vals = words.view(ml_dtypes.float8_e4m3fn if fmt == "e4m3" else ml_dtypes.float8_e5m2).astype(np.float64)
    else:
        nib = np.empty((g, 128, n, 4), np.uint8)
        nib[..., 0::2] = words & 0xF
        nib[..., 1::2] = words >> 4
        vals = E2M1[nib]
    vals = vals * np.repeat(np.exp2(scales.astype(np.float64) - 127.0), 8, axis=1)[..., None]
    return vals.transpose(0, 1, 3, 2).reshape(g * 512, n)


K, T, J, R, C, O, N, Z = 1024, 1024, 256, 512, 1024, 256, 256, 512


def setup_inputs():
    n = np.random.standard_normal
    idx = np.random.permutation(T)[:J]
    idx2 = np.random.permutation(C)[:J]
    idx3 = np.random.permutation(C)[:O]
    idx4 = np.random.permutation(Z)[:O]
    fk = mx_kscale(K)
    fr = mx_kscale(R)
    xtp = pack_weight(n((K, T)) / fk[:, None], "e2m1")
    wp = pack_weight(n((K, R)) * 1 / np.sqrt(K) * fk[:, None] * fr, "e2m1")
    wbp = pack_weight(n((R, N)) * 1 / np.sqrt(R) / fr[:, None], "e5m2")
    return {
        "xt_words": xtp[0],
        "xt_scales": xtp[1],
        "w_words": wp[0],
        "w_scales": wp[1],
        "oldh": (n((R, C)) * 0.7 * fr[:, None]).astype(np.float32),
        "wb_words": wbp[0],
        "wb_scales": wbp[1],
        "tz": (n((N, Z))).astype(np.float32),
        "offs": striped(idx),
        "offs2": striped(idx2),
        "offs3": striped(idx3),
        "offs4": striped(idx4),
    }


def reference(xt_words, xt_scales, w_words, w_scales, oldh, wb_words, wb_scales, tz, offs, offs2, offs3, offs4):
    idx = unstriped(offs)
    idx2 = unstriped(offs2)
    idx3 = unstriped(offs3)
    idx4 = unstriped(offs4)
    xtu = unpack_weight(xt_words, xt_scales, "e2m1")
    wu = unpack_weight(w_words, w_scales, "e2m1")
    wbu = unpack_weight(wb_words, wb_scales, "e5m2")
    xtidxg = xtu[:, idx]
    a = wu.T @ xtidxg
    ha = np.maximum(a, 0.0)
    pw0 = np.zeros((R, C))
    pw0[:, idx2] = ha
    pg = pw0 + f64(oldh)
    hid = pg[:, idx3]
    hidq = mxq(hid, 0, "e5m2")
    p = wbu.T @ hidq
    y = p * f64(tz)[:, idx4]
    return y

@@ -1,0 +1,199 @@
+from contextlib import ExitStack
+
+import concourse.mybir as mybir
+
+K, T, J, R, C, O, N, Z = 1024, 1024, 256, 512, 1024, 256, 256, 512
+FLOPS = 2 * K * R * J + 2 * R * N * O
+
+F32 = mybir.dt.float32
+BF16 = mybir.dt.bfloat16
+I32 = mybir.dt.int32
+U32 = mybir.dt.uint32
+U16 = mybir.dt.uint16
+U8 = mybir.dt.uint8
+FP4X4 = mybir.dt.float4_e2m1fn_x4
+E5M2X4 = mybir.dt.float8_e5m2_x4
+ALU = mybir.AluOpType
+ACT = mybir.ActivationFunctionType
+
+P = 128
+PACK = 4
+PASSES = K // (P * PACK)
+QUADS = 4
+HALVES = N // P
+
+
+def load_scale_rows(queue, plane, scales):
+    passes = scales.shape[0]
+    rows = scales.bitcast(I32)
+    words = plane[:].bitcast(I32).rearrange("p (g c) -> p g c", g=passes)
+    for q in range(QUADS):
+        queue.dma_start(
+            out=words[32 * q : 32 * q + 4],
+            in_=rows[:, 4 * q : 4 * q + 4, :].rearrange("g r c -> r g c"),
+        )
+
+
+def tile_list_page_picked_timeslook_kernel(
+    tc, xt_words, xt_scales, w_words, w_scales, oldh, wb_words, wb_scales, tz, offs, offs2, offs3, offs4, out
+):
+    nc = tc.nc
+    with ExitStack() as ctx:
+        sb = ctx.enter_context(tc.tile_pool(name="sb", bufs=1))
+        ps = ctx.enter_context(tc.psum_pool(name="ps", bufs=1))
+
+        def held(name, shape, dtype):
+            return sb.tile(shape, dtype, name=name, align_bytes=64)
+
+        tok_list = held("tok_list", [P, J // 16], U16)
+        put_list = held("put_list", [P, J // 16], U16)
+        read_list = held("read_list", [P, O // 16], U16)
+        tz_list = held("tz_list", [P, O // 16], U16)
+
+        x_words = [held("x_words%d" % g, [P, T], U16) for g in range(PASSES)]
+        x_plane = held("x_plane", [P, PASSES * T], U8)
+        w_raw = held("w_raw", [P, PASSES * R], U16)
+        w_plane_raw = held("w_plane_raw", [P, PASSES * R], U8)
+        wb_codes = held("wb_codes", [P, N], U32)
+        wb_plane = held("wb_plane", [P, N], U8)
+        old = [held("old%d" % t, [P, C], F32) for t in range(PACK)]
+        put = [held("put%d" % t, [P, C], F32) for t in range(PACK - 1)]
+        put.append(put[1])
+        page = [held("page%d" % t, [P, C], F32) for t in range(PACK)]
+        tz_rows = [held("tz_rows%d" % h, [P, Z], F32) for h in range(HALVES)]
+
+        nc.vector.memset(x_plane[:].bitcast(I32), 0)
+        nc.vector.memset(w_plane_raw[:].bitcast(I32), 0)
+        for t in range(PACK - 1):
+            nc.vector.memset(put[t][:].bitcast(I32), 0)
+        nc.vector.memset(wb_plane[:].bitcast(I32), 0)
+
+        nc.sync.dma_start(out=tok_list[:], in_=offs)
+        nc.sync.dma_start(out=x_words[0][:].bitcast(I32), in_=xt_words[0].bitcast(I32))
+        load_scale_rows(nc.sync, x_plane, xt_scales)
+        nc.sync.dma_start(out=x_words[1][:].bitcast(I32), in_=xt_words[1].bitcast(I32))
+        nc.sync.dma_start(
+            out=w_raw[:].bitcast(I32).rearrange("p (g c) -> p g c", g=PASSES),
+            in_=w_words.bitcast(I32).rearrange("g p c -> p g c"),
+        )
+        load_scale_rows(nc.sync, w_plane_raw, w_scales)
+        nc.sync.dma_start(out=put_list[:], in_=offs2)
+        old_rows = oldh.rearrange("(p t) c -> t p c", t=PACK)
+        for t in range(PACK):
+            nc.sync.dma_start(out=old[t][:], in_=old_rows[t])
+        nc.sync.dma_start(out=read_list[:], in_=offs3)
+        nc.sync.dma_start(out=tz_list[:], in_=offs4)
+        nc.sync.dma_start(
+            out=wb_codes[:].bitcast(I32), in_=wb_words[0].rearrange("p n t -> p (n t)").bitcast(I32)
+        )
+        for h in range(HALVES):
+            nc.sync.dma_start(out=tz_rows[h][:], in_=tz[h * P : (h + 1) * P, :])
+
+        load_scale_rows(nc.sync, wb_plane, wb_scales)
+
+        xg_words = [held("xg_words%d" % g, [P, J], U16) for g in range(PASSES)]
+        xg_plane = [held("xg_plane%d" % g, [P, J], U8) for g in range(PASSES)]
+        for g in range(PASSES):
+            nc.vector.tensor_copy(out=xg_words[g][:], in_=x_words[g][:].indirect(tok_list[:]))
+            nc.vector.tensor_copy(out=xg_plane[g][:], in_=x_plane[:, g * T : (g + 1) * T].indirect(tok_list[:]))
+
+        slot_groups = [(0, 1), (1, 2), (2, PACK)]
+        w_by_slot = w_raw[:].rearrange("p (g m t) -> p g t m", g=PASSES, t=PACK)
+        plane_by_slot = w_plane_raw[:].rearrange("p (g m t) -> p g t m", g=PASSES, t=PACK)
+        bank_tags = ["bank_scalar", "bank_vector", "bank_scalar"]
+
+        def first_product(u):
+            lo, hi = slot_groups[u]
+            w_dealt = held("w_dealt%d" % u, [P, PASSES, hi - lo, P], U16)
+            w_plane = held("w_plane%d" % u, [P, PASSES, hi - lo, P], U8)
+            nc.vector.tensor_copy(out=w_dealt[:], in_=w_by_slot[:, :, lo:hi, :])
+            nc.vector.tensor_copy(out=w_plane[:], in_=plane_by_slot[:, :, lo:hi, :])
+            acc = ps.tile([P, hi - lo, J], F32, name=bank_tags[u])
+            for e in range(hi - lo):
+                for g in range(PASSES):
+                    nc.tensor.matmul_mx(
+                        out=acc[:, e, :],
+                        lhsT=w_dealt[:, g, e, :].bitcast(FP4X4),
+                        lhsT_scale=w_plane[:, g, e, :],
+                        rhs=xg_words[g][:].bitcast(FP4X4),
+                        rhs_scale=xg_plane[g][:],
+                        start=(g == 0),
+                        stop=(g == PASSES - 1),
+                    )
+            return acc
+
+        ha0 = held("ha0", [P, J], F32)
+        ha1 = held("ha1", [P, J], F32)
+        ha23 = held("ha23", [P, 2, J], F32)
+        ha = [ha0[:], ha1[:], ha23[:, 0, :], ha23[:, 1, :]]
+
+        def scatter_on_scalar(t):
+            nc.scalar.activation(out=put[t][:].indirect(put_list[:]), in_=ha[t], func=ACT.Copy)
+
+        def add_old(t):
+            nc.vector.tensor_tensor(out=page[t][:], in0=put[t][:], in1=old[t][:], op=ALU.add)
+
+        def pick_on_scalar(picked, t):
+            nc.scalar.activation(out=picked[:, t, :], in_=page[t][:].indirect(read_list[:]), func=ACT.Copy)
+
+        part_cols = [slice(a * P, (a + 1) * P) for a in range(2)]
+        part_entries = [slice(a * P // 16, (a + 1) * P // 16) for a in range(2)]
+
+        acc0 = first_product(0)
+        acc1 = first_product(1)
+        nc.scalar.activation(out=ha0[:], in_=acc0[:, 0, :], func=ACT.Relu)
+        acc23 = first_product(2)
+        scatter_on_scalar(0)
+        nc.vector.tensor_scalar_max(out=ha1[:], in0=acc1[:, 0, :], scalar1=0.0)
+        nc.vector.tensor_copy(out=put[1][:].indirect(put_list[:]), in_=ha1[:])
+        nc.scalar.activation(out=ha23[:], in_=acc23[:], func=ACT.Relu)
+        scatter_on_scalar(2)
+        add_old(1)
+        scatter_on_scalar(3)
+        add_old(0)
+        add_old(2)
+        add_old(3)
+        picked = held("ha23", [P, PACK, O], F32)
+        for t in range(PACK - 1):
+            pick_on_scalar(picked, t)
+        for a in range(2):
+            nc.vector.tensor_copy(
+                out=picked[:, PACK - 1, part_cols[a]], in_=page[PACK - 1][:].indirect(read_list[:, part_entries[a]])
+            )
+
+        tz_picked = held("page%d" % (PACK - 2), [P, HALVES, O], F32)
+        for h in range(HALVES):
+            nc.scalar.activation(out=tz_picked[:, h, :], in_=tz_rows[h][:].indirect(tz_list[:]), func=ACT.Copy)
+
+        hid = [held("hid%d" % a, [P, P, PACK], BF16) for a in range(2)]
+        hid_codes = [held("hid_codes%d" % a, [P, P], U32) for a in range(2)]
+        hid_plane = [held("hid_plane%d" % a, [P, P], U8) for a in range(2)]
+        for a in range(2):
+            nc.vector.tensor_copy(
+                out=hid[a][:].rearrange("p (c i) t -> p c t i", i=4),
+                in_=picked[:, :, part_cols[a]].rearrange("p t (c i) -> p c t i", i=4),
+            )
+        for a in range(2):
+            nc.vector.quantize_mx(
+                out=hid_codes[a][:].bitcast(E5M2X4),
+                scales=hid_plane[a][:],
+                in_=hid[a][:].rearrange("p o t -> p (o t)"),
+            )
+
+        out_rows = out.rearrange("(h p) o -> p h o", p=P)
+        for a in range(2):
+            prod = ps.tile([P, HALVES, P], F32, name="prod%d" % a)
+            for h in range(HALVES):
+                cols = slice(h * P, (h + 1) * P)
+                nc.tensor.matmul_mx(
+                    out=prod[:, h, :],
+                    lhsT=wb_codes[:, cols].bitcast(E5M2X4),
+                    lhsT_scale=wb_plane[:, cols],
+                    rhs=hid_codes[a][:].bitcast(E5M2X4),
+                    rhs_scale=hid_plane[a][:],
+                    start=True,
+                    stop=True,
+                )
+            result = held("result%d" % a, [P, HALVES, P], F32)
+            nc.vector.tensor_tensor(out=result[:], in0=prod[:], in1=tz_picked[:, :, part_cols[a]], op=ALU.mult)
+            nc.sync.dma_start(out=out_rows[:, :, part_cols[a]], in_=result[:])

@@ -25,13 +25,10 @@ HALVES = N // P
 
 def load_scale_rows(queue, plane, scales):
     passes = scales.shape[0]
-    rows = scales.bitcast(I32)
+    rows = scales.bitcast(I32).rearrange("g (q r) c -> r q g c", r=4)
     words = plane[:].bitcast(I32).rearrange("p (g c) -> p g c", g=passes)
-    for q in range(QUADS):
-        queue.dma_start(
-            out=words[32 * q : 32 * q + 4],
-            in_=rows[:, 4 * q : 4 * q + 4, :].rearrange("g r c -> r g c"),
-        )
+    for r in range(4):
+        queue.dma_start(out=words[r:P:32], in_=rows[r])
 
 
 def tile_list_page_picked_timeslook_kernel(
@@ -58,7 +55,6 @@ def tile_list_page_picked_timeslook_kernel(
         wb_plane = held("wb_plane", [P, N], U8)
         old = [held("old%d" % t, [P, C], F32) for t in range(PACK)]
         put = [held("put%d" % t, [P, C], F32) for t in range(PACK - 1)]
-        put.append(put[1])
         page = [held("page%d" % t, [P, C], F32) for t in range(PACK)]
         tz_rows = [held("tz_rows%d" % h, [P, Z], F32) for h in range(HALVES)]
 
@@ -96,6 +92,9 @@ def tile_list_page_picked_timeslook_kernel(
         for g in range(PASSES):
             nc.vector.tensor_copy(out=xg_words[g][:], in_=x_words[g][:].indirect(tok_list[:]))
             nc.vector.tensor_copy(out=xg_plane[g][:], in_=x_plane[:, g * T : (g + 1) * T].indirect(tok_list[:]))
+
+        put.append(held("x_words0", [P, C], F32))
+        nc.gpsimd.memset(put[PACK - 1][:].bitcast(I32), 0)
 
         slot_groups = [(0, 1), (1, 2), (2, PACK)]
         w_by_slot = w_raw[:].rearrange("p (g m t) -> p g t m", g=PASSES, t=PACK)
@@ -146,13 +145,12 @@ def tile_list_page_picked_timeslook_kernel(
         scatter_on_scalar(0)
         nc.vector.tensor_scalar_max(out=ha1[:], in0=acc1[:, 0, :], scalar1=0.0)
         nc.vector.tensor_copy(out=put[1][:].indirect(put_list[:]), in_=ha1[:])
-        nc.scalar.activation(out=ha23[:], in_=acc23[:], func=ACT.Relu)
+        for e in range(2):
+            nc.scalar.activation(out=ha23[:, e, :], in_=acc23[:, e, :], func=ACT.Relu)
         scatter_on_scalar(2)
-        add_old(1)
         scatter_on_scalar(3)
-        add_old(0)
-        add_old(2)
-        add_old(3)
+        for t in range(PACK):
+            add_old(t)
         picked = held("ha23", [P, PACK, O], F32)
         for t in range(PACK - 1):
             pick_on_scalar(picked, t)

@@ -54,15 +54,20 @@ def tile_list_page_picked_timeslook_kernel(
         wb_codes = held("wb_codes", [P, N], U32)
         wb_plane = held("wb_plane", [P, N], U8)
         old = [held("old%d" % t, [P, C], F32) for t in range(PACK)]
-        put = [held("put%d" % t, [P, C], F32) for t in range(PACK - 1)]
+        put = [held("put%d" % t, [P, C], F32) for t in range(PACK)]
         page = [held("page%d" % t, [P, C], F32) for t in range(PACK)]
         tz_rows = [held("tz_rows%d" % h, [P, Z], F32) for h in range(HALVES)]
 
-        nc.vector.memset(x_plane[:].bitcast(I32), 0)
-        nc.vector.memset(w_plane_raw[:].bitcast(I32), 0)
-        for t in range(PACK - 1):
-            nc.vector.memset(put[t][:].bitcast(I32), 0)
-        nc.vector.memset(wb_plane[:].bitcast(I32), 0)
+        def clear_on_vector(cleared):
+            words = cleared[:].bitcast(I32)
+            cut = words.shape[1] // 2 - 1
+            nc.vector.memset(words[:, :cut], 0)
+            nc.vector.memset(words[:, cut:], 0)
+
+        for cleared in (x_plane, put[0], put[1]):
+            clear_on_vector(cleared)
+        for cleared in (put[2], w_plane_raw, put[3], wb_plane):
+            nc.gpsimd.memset(cleared[:].bitcast(I32), 0)
 
         nc.sync.dma_start(out=tok_list[:], in_=offs)
         nc.sync.dma_start(out=x_words[0][:].bitcast(I32), in_=xt_words[0].bitcast(I32))
@@ -93,9 +98,6 @@ def tile_list_page_picked_timeslook_kernel(
             nc.vector.tensor_copy(out=xg_words[g][:], in_=x_words[g][:].indirect(tok_list[:]))
             nc.vector.tensor_copy(out=xg_plane[g][:], in_=x_plane[:, g * T : (g + 1) * T].indirect(tok_list[:]))
 
-        put.append(held("x_words0", [P, C], F32))
-        nc.gpsimd.memset(put[PACK - 1][:].bitcast(I32), 0)
-
         slot_groups = [(0, 1), (1, 2), (2, PACK)]
         w_by_slot = w_raw[:].rearrange("p (g m t) -> p g t m", g=PASSES, t=PACK)
         plane_by_slot = w_plane_raw[:].rearrange("p (g m t) -> p g t m", g=PASSES, t=PACK)
@@ -121,13 +123,10 @@ def tile_list_page_picked_timeslook_kernel(
                     )
             return acc
 
-        ha0 = held("ha0", [P, J], F32)
-        ha1 = held("ha1", [P, J], F32)
-        ha23 = held("ha23", [P, 2, J], F32)
-        ha = [ha0[:], ha1[:], ha23[:, 0, :], ha23[:, 1, :]]
+        ha = [held("ha%d" % t, [P, J], F32) for t in range(PACK)]
 
         def scatter_on_scalar(t):
-            nc.scalar.activation(out=put[t][:].indirect(put_list[:]), in_=ha[t], func=ACT.Copy)
+            nc.scalar.activation(out=put[t][:].indirect(put_list[:]), in_=ha[t][:], func=ACT.Copy)
 
         def add_old(t):
             nc.vector.tensor_tensor(out=page[t][:], in0=put[t][:], in1=old[t][:], op=ALU.add)
@@ -140,18 +139,18 @@ def tile_list_page_picked_timeslook_kernel(
 
         acc0 = first_product(0)
         acc1 = first_product(1)
-        nc.scalar.activation(out=ha0[:], in_=acc0[:, 0, :], func=ACT.Relu)
+        nc.scalar.activation(out=ha[0][:], in_=acc0[:, 0, :], func=ACT.Relu)
         acc23 = first_product(2)
         scatter_on_scalar(0)
-        nc.vector.tensor_scalar_max(out=ha1[:], in0=acc1[:, 0, :], scalar1=0.0)
-        nc.vector.tensor_copy(out=put[1][:].indirect(put_list[:]), in_=ha1[:])
+        nc.vector.tensor_scalar_max(out=ha[1][:], in0=acc1[:, 0, :], scalar1=0.0)
+        nc.vector.tensor_copy(out=put[1][:].indirect(put_list[:]), in_=ha[1][:])
         for e in range(2):
-            nc.scalar.activation(out=ha23[:, e, :], in_=acc23[:, e, :], func=ACT.Relu)
+            nc.scalar.activation(out=ha[2 + e][:], in_=acc23[:, e, :], func=ACT.Relu)
         scatter_on_scalar(2)
         scatter_on_scalar(3)
         for t in range(PACK):
             add_old(t)
-        picked = held("ha23", [P, PACK, O], F32)
+        picked = held("ha2", [P, PACK, O], F32)
         for t in range(PACK - 1):
             pick_on_scalar(picked, t)
         for a in range(2):

@@ -54,20 +54,13 @@ def tile_list_page_picked_timeslook_kernel(
         wb_codes = held("wb_codes", [P, N], U32)
         wb_plane = held("wb_plane", [P, N], U8)
         old = [held("old%d" % t, [P, C], F32) for t in range(PACK)]
-        put = [held("put%d" % t, [P, C], F32) for t in range(PACK)]
+        put = [held("put%d" % t, [P, C], F32) for t in range(PACK - 1)]
+        put.append(put[1])
         page = [held("page%d" % t, [P, C], F32) for t in range(PACK)]
         tz_rows = [held("tz_rows%d" % h, [P, Z], F32) for h in range(HALVES)]
 
-        def clear_on_vector(cleared):
-            words = cleared[:].bitcast(I32)
-            cut = words.shape[1] // 2 - 1
-            nc.vector.memset(words[:, :cut], 0)
-            nc.vector.memset(words[:, cut:], 0)
-
-        for cleared in (x_plane, put[0], put[1]):
-            clear_on_vector(cleared)
-        for cleared in (put[2], w_plane_raw, put[3], wb_plane):
-            nc.gpsimd.memset(cleared[:].bitcast(I32), 0)
+        for cleared in (x_plane, w_plane_raw, put[0], put[1], put[2], wb_plane):
+            nc.vector.memset(cleared[:].bitcast(I32), 0)
 
         nc.sync.dma_start(out=tok_list[:], in_=offs)
         nc.sync.dma_start(out=x_words[0][:].bitcast(I32), in_=xt_words[0].bitcast(I32))
@@ -147,8 +140,9 @@ def tile_list_page_picked_timeslook_kernel(
         for e in range(2):
             nc.scalar.activation(out=ha[2 + e][:], in_=acc23[:, e, :], func=ACT.Relu)
         scatter_on_scalar(2)
+        add_old(1)
         scatter_on_scalar(3)
-        for t in range(PACK):
+        for t in (0, 2, 3):
             add_old(t)
         picked = held("ha2", [P, PACK, O], F32)
         for t in range(PACK - 1):

from contextlib import ExitStack

import concourse.mybir as mybir

K, T, J, R, C, O, N, Z = 1024, 1024, 256, 512, 1024, 256, 256, 512
FLOPS = 2 * K * R * J + 2 * R * N * O

F32 = mybir.dt.float32
BF16 = mybir.dt.bfloat16
I32 = mybir.dt.int32
U32 = mybir.dt.uint32
U16 = mybir.dt.uint16
U8 = mybir.dt.uint8
FP4X4 = mybir.dt.float4_e2m1fn_x4
E5M2X4 = mybir.dt.float8_e5m2_x4
ALU = mybir.AluOpType
ACT = mybir.ActivationFunctionType

P = 128
PACK = 4
PASSES = K // (P * PACK)
QUADS = 4
HALVES = N // P


def load_scale_rows(queue, plane, scales):
    passes = scales.shape[0]
    rows = scales.bitcast(I32).rearrange("g (q r) c -> r q g c", r=4)
    words = plane[:].bitcast(I32).rearrange("p (g c) -> p g c", g=passes)
    for r in range(4):
        queue.dma_start(out=words[r:P:32], in_=rows[r])


def tile_list_page_picked_timeslook_kernel(
    tc, xt_words, xt_scales, w_words, w_scales, oldh, wb_words, wb_scales, tz, offs, offs2, offs3, offs4, out
):
    nc = tc.nc
    with ExitStack() as ctx:
        sb = ctx.enter_context(tc.tile_pool(name="sb", bufs=1))
        ps = ctx.enter_context(tc.psum_pool(name="ps", bufs=1))

        def held(name, shape, dtype):
            return sb.tile(shape, dtype, name=name, align_bytes=64)

        tok_list = held("tok_list", [P, J // 16], U16)
        put_list = held("put_list", [P, J // 16], U16)
        read_list = held("read_list", [P, O // 16], U16)
        tz_list = held("tz_list", [P, O // 16], U16)

        x_words = [held("x_words%d" % g, [P, T], U16) for g in range(PASSES)]
        x_plane = held("x_plane", [P, PASSES * T], U8)
        w_raw = held("w_raw", [P, PASSES * R], U16)
        w_plane_raw = held("w_plane_raw", [P, PASSES * R], U8)
        wb_codes = held("wb_codes", [P, N], U32)
        wb_plane = held("wb_plane", [P, N], U8)
        old = [held("old%d" % t, [P, C], F32) for t in range(PACK)]
        put = [held("put%d" % t, [P, C], F32) for t in range(PACK - 1)]
        put.append(put[1])
        page = [held("page%d" % t, [P, C], F32) for t in range(PACK)]
        tz_rows = [held("tz_rows%d" % h, [P, Z], F32) for h in range(HALVES)]

        for cleared in (x_plane, w_plane_raw, put[0], put[1], put[2], wb_plane):
            nc.vector.memset(cleared[:].bitcast(I32), 0)

        nc.sync.dma_start(out=tok_list[:], in_=offs)
        nc.sync.dma_start(out=x_words[0][:].bitcast(I32), in_=xt_words[0].bitcast(I32))
        load_scale_rows(nc.sync, x_plane, xt_scales)
        nc.sync.dma_start(out=x_words[1][:].bitcast(I32), in_=xt_words[1].bitcast(I32))
        nc.sync.dma_start(
            out=w_raw[:].bitcast(I32).rearrange("p (g c) -> p g c", g=PASSES),
            in_=w_words.bitcast(I32).rearrange("g p c -> p g c"),
        )
        load_scale_rows(nc.sync, w_plane_raw, w_scales)
        nc.sync.dma_start(out=put_list[:], in_=offs2)
        old_rows = oldh.rearrange("(p t) c -> t p c", t=PACK)
        for t in range(PACK):
            nc.sync.dma_start(out=old[t][:], in_=old_rows[t])
        nc.sync.dma_start(out=read_list[:], in_=offs3)
        nc.sync.dma_start(out=tz_list[:], in_=offs4)
        nc.sync.dma_start(
            out=wb_codes[:].bitcast(I32), in_=wb_words[0].rearrange("p n t -> p (n t)").bitcast(I32)
        )
        for h in range(HALVES):
            nc.sync.dma_start(out=tz_rows[h][:], in_=tz[h * P : (h + 1) * P, :])

        load_scale_rows(nc.sync, wb_plane, wb_scales)

        xg_words = [held("xg_words%d" % g, [P, J], U16) for g in range(PASSES)]
        xg_plane = [held("xg_plane%d" % g, [P, J], U8) for g in range(PASSES)]
        for g in range(PASSES):
            nc.vector.tensor_copy(out=xg_words[g][:], in_=x_words[g][:].indirect(tok_list[:]))
            nc.vector.tensor_copy(out=xg_plane[g][:], in_=x_plane[:, g * T : (g + 1) * T].indirect(tok_list[:]))

        slot_groups = [(0, 1), (1, 2), (2, PACK)]
        w_by_slot = w_raw[:].rearrange("p (g m t) -> p g t m", g=PASSES, t=PACK)
        plane_by_slot = w_plane_raw[:].rearrange("p (g m t) -> p g t m", g=PASSES, t=PACK)
        bank_tags = ["bank_scalar", "bank_vector", "bank_scalar"]

        def first_product(u):
            lo, hi = slot_groups[u]
            w_dealt = held("w_dealt%d" % u, [P, PASSES, hi - lo, P], U16)
            w_plane = held("w_plane%d" % u, [P, PASSES, hi - lo, P], U8)
            nc.vector.tensor_copy(out=w_dealt[:], in_=w_by_slot[:, :, lo:hi, :])
            nc.vector.tensor_copy(out=w_plane[:], in_=plane_by_slot[:, :, lo:hi, :])
            acc = ps.tile([P, hi - lo, J], F32, name=bank_tags[u])
            for e in range(hi - lo):
                for g in range(PASSES):
                    nc.tensor.matmul_mx(
                        out=acc[:, e, :],
                        lhsT=w_dealt[:, g, e, :].bitcast(FP4X4),
                        lhsT_scale=w_plane[:, g, e, :],
                        rhs=xg_words[g][:].bitcast(FP4X4),
                        rhs_scale=xg_plane[g][:],
                        start=(g == 0),
                        stop=(g == PASSES - 1),
                    )
            return acc

        ha = [held("ha%d" % t, [P, J], F32) for t in range(PACK)]

        def scatter_on_scalar(t):
            nc.scalar.activation(out=put[t][:].indirect(put_list[:]), in_=ha[t][:], func=ACT.Copy)

        def add_old(t):
            nc.vector.tensor_tensor(out=page[t][:], in0=put[t][:], in1=old[t][:], op=ALU.add)

        def pick_on_scalar(picked, t):
            nc.scalar.activation(out=picked[:, t, :], in_=page[t][:].indirect(read_list[:]), func=ACT.Copy)

        part_cols = [slice(a * P, (a + 1) * P) for a in range(2)]
        part_entries = [slice(a * P // 16, (a + 1) * P // 16) for a in range(2)]

        acc0 = first_product(0)
        acc1 = first_product(1)
        nc.scalar.activation(out=ha[0][:], in_=acc0[:, 0, :], func=ACT.Relu)
        acc23 = first_product(2)
        scatter_on_scalar(0)
        nc.vector.tensor_scalar_max(out=ha[1][:], in0=acc1[:, 0, :], scalar1=0.0)
        nc.vector.tensor_copy(out=put[1][:].indirect(put_list[:]), in_=ha[1][:])
        for e in range(2):
            nc.scalar.activation(out=ha[2 + e][:], in_=acc23[:, e, :], func=ACT.Relu)
        scatter_on_scalar(2)
        add_old(1)
        scatter_on_scalar(3)
        for t in (0, 2, 3):
            add_old(t)
        picked = held("ha2", [P, PACK, O], F32)
        for t in range(PACK - 1):
            pick_on_scalar(picked, t)
        for a in range(2):
            nc.vector.tensor_copy(
                out=picked[:, PACK - 1, part_cols[a]], in_=page[PACK - 1][:].indirect(read_list[:, part_entries[a]])
            )

        tz_picked = held("page%d" % (PACK - 2), [P, HALVES, O], F32)
        for h in range(HALVES):
            nc.scalar.activation(out=tz_picked[:, h, :], in_=tz_rows[h][:].indirect(tz_list[:]), func=ACT.Copy)

        hid = [held("hid%d" % a, [P, P, PACK], BF16) for a in range(2)]
        hid_codes = [held("hid_codes%d" % a, [P, P], U32) for a in range(2)]
        hid_plane = [held("hid_plane%d" % a, [P, P], U8) for a in range(2)]
        for a in range(2):
            nc.vector.tensor_copy(
                out=hid[a][:].rearrange("p (c i) t -> p c t i", i=4),
                in_=picked[:, :, part_cols[a]].rearrange("p t (c i) -> p c t i", i=4),
            )
        for a in range(2):
            nc.vector.quantize_mx(
                out=hid_codes[a][:].bitcast(E5M2X4),
                scales=hid_plane[a][:],
                in_=hid[a][:].rearrange("p o t -> p (o t)"),
            )

        out_rows = out.rearrange("(h p) o -> p h o", p=P)
        for a in range(2):
            prod = ps.tile([P, HALVES, P], F32, name="prod%d" % a)
            for h in range(HALVES):
                cols = slice(h * P, (h + 1) * P)
                nc.tensor.matmul_mx(
                    out=prod[:, h, :],
                    lhsT=wb_codes[:, cols].bitcast(E5M2X4),
                    lhsT_scale=wb_plane[:, cols],
                    rhs=hid_codes[a][:].bitcast(E5M2X4),
                    rhs_scale=hid_plane[a][:],
                    start=True,
                    stop=True,
                )
            result = held("result%d" % a, [P, HALVES, P], F32)
            nc.vector.tensor_tensor(out=result[:], in0=prod[:], in1=tz_picked[:, :, part_cols[a]], op=ALU.mult)
            nc.sync.dma_start(out=out_rows[:, :, part_cols[a]], in_=result[:])
